import numpy as np
import ml_dtypes


def mxq(x, axis, fmt="e4m3"):
    dtype, down = {"e4m3": (ml_dtypes.float8_e4m3fn, 7), "e5m2": (ml_dtypes.float8_e5m2, 14)}[fmt]
    v = np.moveaxis(np.asarray(x, np.float32).astype(ml_dtypes.bfloat16).astype(np.float64), axis, -1)
    blocks = v.reshape(v.shape[:-1] + (-1, 32))
    amax = np.abs(blocks).max(-1, keepdims=True)
    byte = np.maximum(np.where(amax > 0, np.frexp(amax)[1] - 1 + 127, 0) - down, 1)
    scale = np.exp2(byte - 127.0)
    codes = (blocks / scale).astype(np.float32).astype(dtype).astype(np.float64)
    return np.moveaxis((codes * scale).reshape(v.shape), -1, axis)


WIDE = False


def mx_kscale(k):
    if not WIDE:
        return np.ones(k)
    levels = np.array([10, -10, 5, -5, 0])
    if k % 512:
        return np.exp2(np.random.permutation(np.resize(levels, k // 32))).repeat(32)
    a = np.empty((k // 512, 16))
    for p in range(k // 512):
        a[p, :8] = np.random.permutation(np.resize(levels, 8))
        for g in range(8):
            far = levels[np.abs(levels - a[p, g]) >= 10]
            a[p, g + 8] = far[np.random.randint(len(far))]
    return np.exp2(a.ravel()).repeat(32)


def f64(x):
    return np.asarray(x).astype(np.float64)


def striped(idx):
    return np.tile(idx.reshape(-1, 16).T, (8, 1)).astype(np.uint16)


def unstriped(offs):
    return offs[:16].T.reshape(-1).astype(np.int64)


E2M1 = np.array([0.0, 0.5, 1.0, 1.5, 2.0, 3.0, 4.0, 6.0, -0.0, -0.5, -1.0, -1.5, -2.0, -3.0, -4.0, -6.0])


def pack_weight(w, fmt):
    k, n = w.shape
    w = f64(np.asarray(w, np.float32).astype(ml_dtypes.bfloat16)).reshape(k // 32, 32, n)
    amax = np.abs(w).max(1)
    if fmt == "e4m3":
        byte = np.frexp(amax)[1] - 1 + 127 - 7
    else:
        mant, ex = np.frexp(amax / 6.0)
        byte = np.where(mant > 0.5, ex, ex - 1) + 127
    byte = np.clip(np.where(amax > 0, byte, 1), 1, 254)
    scaled = (w * np.exp2(127.0 - byte)[:, None, :]).reshape(k, n).astype(np.float32)
    by_word = np.ascontiguousarray(scaled.reshape(k // 512, 128, 4, n).transpose(0, 1, 3, 2))
    if fmt == "e4m3":
        words = by_word.astype(ml_dtypes.float8_e4m3fn).view(np.uint8)
    else:
        c = by_word.astype(ml_dtypes.float4_e2m1fn).view(np.uint8) & 0xF
        words = (c[..., 0::2] | (c[..., 1::2] << 4)).reshape(k // 512, 128, 2 * n)
    return np.ascontiguousarray(words), np.ascontiguousarray(byte.astype(np.uint8).reshape(k // 512, 16, n))


def unpack_weight(words, scales, fmt):
    g, _, n = scales.shape
    words = np.ascontiguousarray(words).reshape(g, 128, n, -1)
    if fmt == "e4m3":
        vals = words.view(ml_dtypes.float8_e4m3fn).astype(np.float64)
    else:
        nib = np.empty((g, 128, n, 4), np.uint8)
        nib[..., 0::2] = words & 0xF
        nib[..., 1::2] = words >> 4
        vals = E2M1[nib]
    vals = vals * np.repeat(np.exp2(scales.astype(np.float64) - 127.0), 8, axis=1)[..., None]
    return vals.transpose(0, 1, 3, 2).reshape(g * 512, n)


def gelu(v):
    return 0.5 * v * (1.0 + np.tanh(np.sqrt(2.0 / np.pi) * (v + 0.044715 * v**3)))


K, H, T, S, S2, T3, P = 1024, 1024, 4096, 1024, 512, 2048, 512

def setup_inputs():
    n = np.random.standard_normal
    s = mx_kscale(K)[:, None]
    u = mx_kscale(H)[:, None]
    tab_words, tab_scales = pack_weight(n((K, T)) * s, "e4m3")
    tab2_words, tab2_scales = pack_weight(0.57 * n((H, T3)) / np.sqrt(H) / u, "e4m3")
    keep = np.eye(K, H) + 0.3 * n((K, H)) / np.sqrt(K)
    w4_words, w4_scales = pack_weight(keep * u.T / s, "e4m3")
    return {
        "tab_words": tab_words, "tab_scales": tab_scales,
        "offs": striped(np.random.permutation(T)[:S]),
        "tab2_words": tab2_words, "tab2_scales": tab2_scales,
        "offs2": striped(np.random.permutation(T3)[:S2]),
        "pos1": striped(np.random.permutation(S)[:P]),
        "pos2": striped(np.random.permutation(S)[:P]),
        "w1": (1.3 * n((K, H)) / np.sqrt(K) / s).astype(np.float32),
        "w4_words": w4_words, "w4_scales": w4_scales,
        "gain": (np.random.uniform(0.7, 1.6, H) * u[:, 0]).astype(np.float32),
        "temp": np.random.uniform(0.4, 1.6, S2).astype(np.float32),
        "fam": (0.15 * n(S2)).astype(np.float32),
    }

def reference(tab_words, tab_scales, offs, tab2_words, tab2_scales, offs2, pos1, pos2,
              w1, w4_words, w4_scales, gain, temp, fam):
    v = unpack_weight(tab_words, tab_scales, "e4m3")[:, unstriped(offs)]
    v2 = unpack_weight(tab2_words, tab2_scales, "e4m3")[:, unstriped(offs2)]
    w4 = unpack_weight(w4_words, w4_scales, "e4m3")
    spell = np.tanh(mxq(f64(w1), 0, "e4m3").T @ v)
    h = f64(gain)[:, None] * spell + (w4.T @ v)
    e = v2.T @ mxq(h, 0, "e4m3")
    top = e.max(axis=1)
    a = np.exp(f64(temp)[:, None] * (e[:, unstriped(pos1)] - top[:, None]))
    c = e[:, unstriped(pos2)]
    return np.abs(a * c + f64(fam)[:, None])

@@ -1,0 +1,261 @@
+from contextlib import ExitStack
+
+import concourse.mybir as mybir
+
+K, H, T, S, S2, T3, NP = 1024, 1024, 4096, 1024, 512, 2048, 512
+FLOPS = 2 * K * H * S * 2 + 2 * H * S2 * S
+
+F32 = mybir.dt.float32
+BF16 = mybir.dt.bfloat16
+I32 = mybir.dt.int32
+U32 = mybir.dt.uint32
+U16 = mybir.dt.uint16
+U8 = mybir.dt.uint8
+FP8X4 = mybir.dt.float8_e4m3fn_x4
+ACT = mybir.ActivationFunctionType
+ALU = mybir.AluOpType
+
+P = 128
+PACK = 4
+PASS = P * PACK
+HALF = 512
+LIST = 16
+
+CAST_VECTOR_SLOTS = {(0, 0): 0, (0, 1): 0, (1, 0): 2, (1, 1): 2}
+WEAVE_PIECE = 256
+WEAVE_VECTOR_PIECES = {(0, 0): 0, (0, 1): 0, (1, 0): 1, (1, 1): 1}
+
+
+def tile_list_surname_variant_looks_kernel(
+    tc, tab_words, tab_scales, offs, tab2_words, tab2_scales, offs2, pos1, pos2,
+    w1, w4_words, w4_scales, gain, temp, fam, out,
+):
+    nc = tc.nc
+    with ExitStack() as ctx:
+        keep = ctx.enter_context(tc.tile_pool(name="keep", bufs=1))
+        ring = ctx.enter_context(tc.tile_pool(name="ring", bufs=2))
+        psum = ctx.enter_context(tc.psum_pool(name="psum", bufs=1))
+
+        def held(shape, dtype, name):
+            return keep.tile(shape, dtype, name=name, align_bytes=64)
+
+        offs_sb = keep.tile([P, S // LIST], U16, name="offs_sb")
+        offs2_sb = keep.tile([P, S2 // LIST], U16, name="offs2_sb")
+        pos1_sb = keep.tile([P, NP // LIST], U16, name="pos1_sb")
+        pos2_sb = keep.tile([P, NP // LIST], U16, name="pos2_sb")
+        gain_sb = held([P, 2, PACK], F32, "gain_sb")
+        temp_sb = held([P, 4], F32, "temp_sb")
+        fam_sb = held([P, 4], F32, "fam_sb")
+
+        tab_w = [held([P, T], U32, f"tab_w{a}") for a in range(2)]
+        tab_s = held([P, T], U8, "tab_s")
+        tab2_w = [held([P, T3], U32, f"tab2_w{a}") for a in range(2)]
+        tab2_s = held([P, T3], U8, "tab2_s")
+        w4_raw = [held([P, 2, PASS], I32, f"w4_raw{b}") for b in range(2)]
+        w4_raw_s = held([P, H], U8, "w4_raw_s")
+        w1_raw = {(b, a): held([P, PACK, PASS], F32, f"w1_raw{b}{a}") for b in range(2) for a in range(2)}
+
+        for plane in (tab_s, w4_raw_s, tab2_s):
+            nc.vector.memset(plane[:].bitcast(I32), 0)
+
+        def load_scales(plane, scales):
+            for q in range(4):
+                nc.sync.dma_start(
+                    out=plane[32 * q : 32 * q + 8, :].bitcast(I32),
+                    in_=scales[:, 4 * q : 4 * q + 4, :].bitcast(I32),
+                )
+
+        def load_words(tile, words, a):
+            nc.sync.dma_start(
+                out=tile[:].bitcast(I32), in_=words[a].rearrange("p t i -> p (t i)").bitcast(I32)
+            )
+
+        def load_w1(b, a):
+            rows = w1[a * PASS : (a + 1) * PASS, b * PASS : (b + 1) * PASS]
+            nc.sync.dma_start(out=w1_raw[b, a][:], in_=rows.rearrange("(p j) c -> p j c", j=PACK))
+
+        def load_w4(b):
+            words = w4_words.rearrange("a p c i -> p a (c i)")
+            nc.sync.dma_start(
+                out=w4_raw[b][:], in_=words[:, :, b * PASS * 4 : (b + 1) * PASS * 4].bitcast(I32)
+            )
+
+        nc.sync.dma_start(offs_sb[:], offs)
+        load_w1(0, 0)
+        load_scales(tab_s, tab_scales)
+        load_w1(0, 1)
+        nc.sync.dma_start(offs2_sb[:], offs2)
+        load_scales(w4_raw_s, w4_scales)
+        load_words(tab_w[0], tab_words, 0)
+        load_scales(tab2_s, tab2_scales)
+        load_w4(0)
+        load_words(tab_w[1], tab_words, 1)
+        nc.sync.dma_start(out=gain_sb[:], in_=gain.rearrange("(b p t) -> p b t", b=2, t=PACK))
+        load_w1(1, 0)
+        load_w1(1, 1)
+        load_w4(1)
+        load_words(tab2_w[0], tab2_words, 0)
+        load_words(tab2_w[1], tab2_words, 1)
+        nc.sync.dma_start(pos1_sb[:], pos1)
+        nc.sync.dma_start(pos2_sb[:], pos2)
+        with nc.allow_non_contiguous_dma(reason="one value a partition"):
+            nc.sync.dma_start(out=temp_sb[:], in_=temp.rearrange("(c p) -> p c", p=P))
+            nc.sync.dma_start(out=fam_sb[:], in_=fam.rearrange("(c p) -> p c", p=P))
+
+        def entries(half):
+            return offs_sb[:, half * HALF // LIST : (half + 1) * HALF // LIST]
+
+        v_w = {(a, half): held([P, HALF], U32, f"v_w{a}{half}") for a in range(2) for half in range(2)}
+        v_s = [held([P, HALF], U8, f"v_s{half}") for half in range(2)]
+        v2_w = [held([P, S2], U32, f"v2_w{a}") for a in range(2)]
+        v2_s = held([P, S2], U8, "v2_s")
+
+        w4_s = held([P, H], U8, "w4_s")
+
+        def gather_words(a):
+            for half in range(2):
+                nc.vector.tensor_copy(v_w[a, half][:], tab_w[a][:].indirect(entries(half)))
+
+        def deal_w4_scales():
+            nc.vector.tensor_copy(
+                out=w4_s[:].rearrange("p (b t m) -> p b t m", b=2, t=PACK),
+                in_=w4_raw_s[:].rearrange("p (b m t) -> p b t m", b=2, t=PACK),
+            )
+
+        w1_q = {key: held([P, PASS], U32, f"w1_q{key[0]}{key[1]}") for key in w1_raw}
+        w1_s = {key: held([P, PASS], U8, f"w1_s{key[0]}{key[1]}") for key in w1_raw}
+        w4_q = [held([P, 2, PASS], I32, f"w4_q{b}") for b in range(2)]
+
+        def quantize_w1(b, a):
+            grouped = ring.tile([P, PASS * PACK], BF16, name="w1_grouped", align_bytes=64)
+            dst = grouped[:].rearrange("p (t m j) -> p m j t", t=PACK, j=PACK)
+            src = w1_raw[b, a][:].rearrange("p j (m t) -> p m j t", t=PACK)
+            cut = PACK - CAST_VECTOR_SLOTS[b, a]
+            if cut > 0:
+                nc.scalar.copy(out=dst[:, :, :, :cut], in_=src[:, :, :, :cut])
+            if cut < PACK:
+                nc.vector.tensor_copy(out=dst[:, :, :, cut:], in_=src[:, :, :, cut:])
+            nc.vector.quantize_mx(out=w1_q[b, a][:].bitcast(FP8X4), scales=w1_s[b, a][:], in_=grouped[:])
+
+        def deal_w4(b):
+            nc.vector.tensor_copy(
+                out=w4_q[b][:].rearrange("p a (t c i) -> p a c t i", t=PACK, i=4),
+                in_=w4_raw[b][:].rearrange("p a (c i t) -> p a c t i", t=PACK, i=4),
+            )
+
+        h_rows = {}
+        h_q = {(b, half): held([P, HALF], U32, f"h_q{b}{half}") for b in range(2) for half in range(2)}
+        h_s = {(b, half): held([P, HALF], U8, f"h_s{b}{half}") for b in range(2) for half in range(2)}
+
+        def first_stage(b, half):
+            rows = ring.tile([P, PACK, HALF], BF16, name="h_rows", bufs=4, align_bytes=64)
+            h_rows[b, half] = rows
+            for t in range(PACK):
+                cols = slice(t * P, (t + 1) * P)
+                spell = psum.tile([P, HALF], F32, name="spell", bufs=3)
+                for a in range(2):
+                    nc.tensor.matmul_mx(
+                        out=spell[:],
+                        lhsT=w1_q[b, a][:, cols].bitcast(FP8X4), lhsT_scale=w1_s[b, a][:, cols],
+                        rhs=v_w[a, half][:].bitcast(FP8X4), rhs_scale=v_s[half][4 * a :, :],
+                        start=(a == 0), stop=(a == 1),
+                    )
+                resid = psum.tile([P, HALF], F32, name="resid", tag="late", bufs=5)
+                for a in range(2):
+                    nc.tensor.matmul_mx(
+                        out=resid[:],
+                        lhsT=w4_q[b][:, a, cols].bitcast(FP8X4),
+                        lhsT_scale=w4_s[4 * a :, b * PASS + t * P : b * PASS + (t + 1) * P],
+                        rhs=v_w[a, half][:].bitcast(FP8X4), rhs_scale=v_s[half][4 * a :, :],
+                        start=(a == 0), stop=(a == 1),
+                    )
+                bent = ring.tile([P, HALF], F32, name="bent", bufs=3)
+                nc.scalar.activation(out=bent[:], in_=spell[:], func=ACT.Tanh)
+                nc.vector.scalar_tensor_tensor(
+                    out=rows[:, t, :], in0=bent[:], scalar=gain_sb[:, b, t : t + 1], in1=resid[:],
+                    op0=ALU.mult, op1=ALU.add,
+                )
+
+        def quantize_h(b, half):
+            woven = ring.tile([P, HALF * PACK], BF16, name="woven", align_bytes=64)
+            dst = woven[:].rearrange("p (c i t) -> p c t i", t=PACK, i=4)
+            src = h_rows[b, half][:].rearrange("p t (c i) -> p c t i", i=4)
+            pieces = HALF // WEAVE_PIECE
+            for piece in range(pieces):
+                cols = slice(piece * WEAVE_PIECE // 4, (piece + 1) * WEAVE_PIECE // 4)
+                if piece < pieces - WEAVE_VECTOR_PIECES[b, half]:
+                    nc.scalar.copy(out=dst[:, cols], in_=src[:, cols])
+                else:
+                    nc.vector.tensor_copy(out=dst[:, cols], in_=src[:, cols])
+            nc.vector.quantize_mx(out=h_q[b, half][:].bitcast(FP8X4), scales=h_s[b, half][:], in_=woven[:])
+
+        scores = [held([P, S], F32, f"scores{c}") for c in range(4)]
+        top = held([P, 4, 2], F32, "top")
+        neg_temp = held([P, 4], F32, "neg_temp")
+        bias = held([P, 4], F32, "bias")
+
+        def second_stage(c, half):
+            cols = slice(c * P, (c + 1) * P)
+            score = psum.tile([P, HALF], F32, name="score", tag="late", bufs=5)
+            for b in range(2):
+                nc.tensor.matmul_mx(
+                    out=score[:],
+                    lhsT=v2_w[b][:, cols].bitcast(FP8X4), lhsT_scale=v2_s[4 * b :, cols],
+                    rhs=h_q[b, half][:].bitcast(FP8X4), rhs_scale=h_s[b, half][:],
+                    start=(b == 0), stop=(b == 1),
+                )
+            nc.vector.tensor_scalar(
+                out=scores[c][:, half * HALF : (half + 1) * HALF], in0=score[:],
+                scalar1=1.0, scalar2=(top[:, c, 0:1] if half == 1 else None),
+                op0=ALU.mult, op1=ALU.max, accum_out=top[:, c, half : half + 1],
+            )
+
+        def looks(c):
+            nc.scalar.activation(
+                out=bias[:, c : c + 1], in_=top[:, c, 1:2], func=ACT.Copy, scale=neg_temp[:, c : c + 1]
+            )
+            latin = ring.tile([P, NP], F32, name="latin", bufs=4)
+            nc.scalar.activation(
+                out=latin[:], in_=scores[c][:].indirect(pos1_sb[:]), func=ACT.Exp,
+                bias=bias[:, c : c + 1], scale=temp_sb[:, c : c + 1],
+            )
+            return latin
+
+        def finish(c, latin):
+            weighted = ring.tile([P, NP], F32, name="weighted", bufs=4)
+            nc.vector.tensor_tensor(weighted[:], scores[c][:].indirect(pos2_sb[:]), latin[:], ALU.mult)
+            result = ring.tile([P, NP], F32, name="result", bufs=4)
+            nc.scalar.activation(out=result[:], in_=weighted[:], func=ACT.Abs, bias=fam_sb[:, c : c + 1])
+            nc.sync.dma_start(out=out[c * P : (c + 1) * P, :], in_=result[:])
+
+        for half in range(2):
+            nc.vector.tensor_copy(v_s[half][:], tab_s[:].indirect(entries(half)))
+        quantize_w1(0, 0)
+        quantize_w1(0, 1)
+        deal_w4_scales()
+        gather_words(0)
+        deal_w4(0)
+        nc.vector.tensor_copy(v2_s[:], tab2_s[:].indirect(offs2_sb[:]))
+        gather_words(1)
+        first_stage(0, 0)
+        quantize_w1(1, 0)
+        quantize_w1(1, 1)
+        deal_w4(1)
+        first_stage(0, 1)
+        first_stage(1, 0)
+        first_stage(1, 1)
+        quantize_h(0, 0)
+        quantize_h(1, 0)
+        for a in range(2):
+            nc.vector.tensor_copy(v2_w[a][:], tab2_w[a][:].indirect(offs2_sb[:]))
+        nc.vector.tensor_scalar(
+            out=neg_temp[:], in0=temp_sb[:], scalar1=-1.0, scalar2=None, op0=ALU.mult
+        )
+        quantize_h(0, 1)
+        quantize_h(1, 1)
+        for half in range(2):
+            for c in range(4):
+                second_stage(c, half)
+        latins = [looks(c) for c in range(4)]
+        for c in range(4):
+            finish(c, latins[c])

@@ -21,7 +21,8 @@ PASS = P * PACK
 HALF = 512
 LIST = 16
 
-CAST_VECTOR_SLOTS = {(0, 0): 0, (0, 1): 0, (1, 0): 2, (1, 1): 2}
+CAST_VECTOR_SLOTS = {(0, 0): 0, (0, 1): 0, (1, 0): 4, (1, 1): 0}
+SPELL_BANKS, LATE_BANKS = 3, 5
 WEAVE_PIECE = 256
 WEAVE_VECTOR_PIECES = {(0, 0): 0, (0, 1): 0, (1, 0): 1, (1, 1): 1}
 
@@ -55,19 +56,30 @@ def tile_list_surname_variant_looks_kernel(
         w4_raw_s = held([P, H], U8, "w4_raw_s")
         w1_raw = {(b, a): held([P, PACK, PASS], F32, f"w1_raw{b}{a}") for b in range(2) for a in range(2)}
 
-        for plane in (tab_s, w4_raw_s, tab2_s):
+        v_s = held([P, S], U8, "v_s")
+        v2_s = held([P, S2], U8, "v2_s")
+        for plane in (tab_s, w4_raw_s, tab2_s, v_s, v2_s):
             nc.vector.memset(plane[:].bitcast(I32), 0)
 
-        def load_scales(plane, scales):
+        def load_spread_scales(window, scales):
             for q in range(4):
                 nc.sync.dma_start(
-                    out=plane[32 * q : 32 * q + 8, :].bitcast(I32),
+                    out=window[32 * q : 32 * q + 32 : 4, :].bitcast(I32),
                     in_=scales[:, 4 * q : 4 * q + 4, :].bitcast(I32),
                 )
 
-        def load_words(tile, words, a):
+        def close_up_scales(plane, spread):
+            for q in range(4):
+                nc.gpsimd.dma_start(
+                    out=plane[32 * q : 32 * q + 8, :].bitcast(I32),
+                    in_=spread[32 * q : 32 * q + 32 : 4, :].bitcast(I32),
+                )
+
+        def load_words(tile, words, a, first=0, last=None):
+            last = tile.shape[1] if last is None else last
             nc.sync.dma_start(
-                out=tile[:].bitcast(I32), in_=words[a].rearrange("p t i -> p (t i)").bitcast(I32)
+                out=tile[:, first:last].bitcast(I32),
+                in_=words[a, :, first:last].rearrange("p t i -> p (t i)").bitcast(I32),
             )
 
         def load_w1(b, a):
@@ -80,16 +92,21 @@ def tile_list_surname_variant_looks_kernel(
                 out=w4_raw[b][:], in_=words[:, :, b * PASS * 4 : (b + 1) * PASS * 4].bitcast(I32)
             )
 
+        for q in range(4):
+            nc.gpsimd.dma_start(
+                out=w4_raw_s[32 * q : 32 * q + 8, :].bitcast(I32),
+                in_=w4_scales[:, 4 * q : 4 * q + 4, :].bitcast(I32),
+            )
         nc.sync.dma_start(offs_sb[:], offs)
         load_w1(0, 0)
-        load_scales(tab_s, tab_scales)
-        load_w1(0, 1)
+        load_spread_scales(tab_s, tab_scales)
         nc.sync.dma_start(offs2_sb[:], offs2)
-        load_scales(w4_raw_s, w4_scales)
+        load_w1(0, 1)
+        load_spread_scales(tab2_s, tab2_scales)
         load_words(tab_w[0], tab_words, 0)
-        load_scales(tab2_s, tab2_scales)
+        load_words(tab_w[1], tab_words, 1, 0, T // 2)
         load_w4(0)
-        load_words(tab_w[1], tab_words, 1)
+        load_words(tab_w[1], tab_words, 1, T // 2, T)
         nc.sync.dma_start(out=gain_sb[:], in_=gain.rearrange("(b p t) -> p b t", b=2, t=PACK))
         load_w1(1, 0)
         load_w1(1, 1)
@@ -106,9 +123,9 @@ def tile_list_surname_variant_looks_kernel(
             return offs_sb[:, half * HALF // LIST : (half + 1) * HALF // LIST]
 
         v_w = {(a, half): held([P, HALF], U32, f"v_w{a}{half}") for a in range(2) for half in range(2)}
-        v_s = [held([P, HALF], U8, f"v_s{half}") for half in range(2)]
+        v_spread = held([P, S], U8, "v_spread")
         v2_w = [held([P, S2], U32, f"v2_w{a}") for a in range(2)]
-        v2_s = held([P, S2], U8, "v2_s")
+        v2_spread = held([P, S2], U8, "v2_spread")
 
         w4_s = held([P, H], U8, "w4_s")
 
@@ -147,28 +164,49 @@ def tile_list_surname_variant_looks_kernel(
         h_q = {(b, half): held([P, HALF], U32, f"h_q{b}{half}") for b in range(2) for half in range(2)}
         h_s = {(b, half): held([P, HALF], U8, f"h_s{b}{half}") for b in range(2) for half in range(2)}
 
+        def spell_pass(bank, b, half, t, a):
+            cols = slice(t * P, (t + 1) * P)
+            nc.tensor.matmul_mx(
+                out=bank[:],
+                lhsT=w1_q[b, a][:, cols].bitcast(FP8X4), lhsT_scale=w1_s[b, a][:, cols],
+                rhs=v_w[a, half][:].bitcast(FP8X4),
+                rhs_scale=v_s[4 * a :, half * HALF : (half + 1) * HALF],
+                start=(a == 0), stop=(a == 1),
+            )
+
+        def resid_pass(bank, b, half, t, a):
+            nc.tensor.matmul_mx(
+                out=bank[:],
+                lhsT=w4_q[b][:, a, t * P : (t + 1) * P].bitcast(FP8X4),
+                lhsT_scale=w4_s[4 * a :, b * PASS + t * P : b * PASS + (t + 1) * P],
+                rhs=v_w[a, half][:].bitcast(FP8X4),
+                rhs_scale=v_s[4 * a :, half * HALF : (half + 1) * HALF],
+                start=(a == 0), stop=(a == 1),
+            )
+
+        spell_open, resid_open = {}, {}
+
+        def open_spell(key):
+            spell_open[key] = psum.tile([P, HALF], F32, name="spell", bufs=SPELL_BANKS)
+            spell_pass(spell_open[key], *key, 0)
+
+        def open_resid(key):
+            resid_open[key] = psum.tile([P, HALF], F32, name="resid", tag="late", bufs=LATE_BANKS)
+            resid_pass(resid_open[key], *key, 0)
+
         def first_stage(b, half):
             rows = ring.tile([P, PACK, HALF], BF16, name="h_rows", bufs=4, align_bytes=64)
             h_rows[b, half] = rows
             for t in range(PACK):
-                cols = slice(t * P, (t + 1) * P)
-                spell = psum.tile([P, HALF], F32, name="spell", bufs=3)
-                for a in range(2):
-                    nc.tensor.matmul_mx(
-                        out=spell[:],
-                        lhsT=w1_q[b, a][:, cols].bitcast(FP8X4), lhsT_scale=w1_s[b, a][:, cols],
-                        rhs=v_w[a, half][:].bitcast(FP8X4), rhs_scale=v_s[half][4 * a :, :],
-                        start=(a == 0), stop=(a == 1),
-                    )
-                resid = psum.tile([P, HALF], F32, name="resid", tag="late", bufs=5)
-                for a in range(2):
-                    nc.tensor.matmul_mx(
-                        out=resid[:],
-                        lhsT=w4_q[b][:, a, cols].bitcast(FP8X4),
-                        lhsT_scale=w4_s[4 * a :, b * PASS + t * P : b * PASS + (t + 1) * P],
-                        rhs=v_w[a, half][:].bitcast(FP8X4), rhs_scale=v_s[half][4 * a :, :],
-                        start=(a == 0), stop=(a == 1),
-                    )
+                key = (b, half, t)
+                if key not in spell_open:
+                    open_spell(key)
+                spell = spell_open[key]
+                spell_pass(spell, *key, 1)
+                if key not in resid_open:
+                    open_resid(key)
+                resid = resid_open[key]
+                resid_pass(resid, *key, 1)
                 bent = ring.tile([P, HALF], F32, name="bent", bufs=3)
                 nc.scalar.activation(out=bent[:], in_=spell[:], func=ACT.Tanh)
                 nc.vector.scalar_tensor_tensor(
@@ -191,12 +229,11 @@ def tile_list_surname_variant_looks_kernel(
 
         scores = [held([P, S], F32, f"scores{c}") for c in range(4)]
         top = held([P, 4, 2], F32, "top")
-        neg_temp = held([P, 4], F32, "neg_temp")
         bias = held([P, 4], F32, "bias")
 
         def second_stage(c, half):
             cols = slice(c * P, (c + 1) * P)
-            score = psum.tile([P, HALF], F32, name="score", tag="late", bufs=5)
+            score = psum.tile([P, HALF], F32, name="score", tag="late", bufs=LATE_BANKS)
             for b in range(2):
                 nc.tensor.matmul_mx(
                     out=score[:],
@@ -211,8 +248,9 @@ def tile_list_surname_variant_looks_kernel(
             )
 
         def looks(c):
-            nc.scalar.activation(
-                out=bias[:, c : c + 1], in_=top[:, c, 1:2], func=ACT.Copy, scale=neg_temp[:, c : c + 1]
+            nc.gpsimd.tensor_scalar(
+                out=bias[:, c : c + 1], in0=top[:, c, 1:2], scalar1=temp_sb[:, c : c + 1], scalar2=-1.0,
+                op0=ALU.mult, op1=ALU.mult,
             )
             latin = ring.tile([P, NP], F32, name="latin", bufs=4)
             nc.scalar.activation(
@@ -222,35 +260,43 @@ def tile_list_surname_variant_looks_kernel(
             return latin
 
         def finish(c, latin):
-            weighted = ring.tile([P, NP], F32, name="weighted", bufs=4)
-            nc.vector.tensor_tensor(weighted[:], scores[c][:].indirect(pos2_sb[:]), latin[:], ALU.mult)
-            result = ring.tile([P, NP], F32, name="result", bufs=4)
-            nc.scalar.activation(out=result[:], in_=weighted[:], func=ACT.Abs, bias=fam_sb[:, c : c + 1])
-            nc.sync.dma_start(out=out[c * P : (c + 1) * P, :], in_=result[:])
+            pieces = 2 if c == 3 else 1
+            width = NP // pieces
+            for piece in range(pieces):
+                cols = slice(piece * width, (piece + 1) * width)
+                picks = pos2_sb[:, piece * width // LIST : (piece + 1) * width // LIST]
+                weighted = ring.tile([P, width], F32, name="weighted", bufs=4)
+                nc.vector.tensor_tensor(weighted[:], scores[c][:].indirect(picks), latin[:, cols], ALU.mult)
+                result = ring.tile([P, width], F32, name="result", bufs=5)
+                nc.scalar.activation(out=result[:], in_=weighted[:], func=ACT.Abs, bias=fam_sb[:, c : c + 1])
+                nc.sync.dma_start(out=out[c * P : (c + 1) * P, cols], in_=result[:])
 
-        for half in range(2):
-            nc.vector.tensor_copy(v_s[half][:], tab_s[:].indirect(entries(half)))
+        nc.vector.tensor_copy(v_spread[:], tab_s[:].indirect(offs_sb[:]))
+        close_up_scales(v_s, v_spread)
         quantize_w1(0, 0)
         quantize_w1(0, 1)
-        deal_w4_scales()
+        nc.vector.tensor_copy(v2_spread[:], tab2_s[:].indirect(offs2_sb[:]))
+        close_up_scales(v2_s, v2_spread)
         gather_words(0)
+        deal_w4_scales()
         deal_w4(0)
-        nc.vector.tensor_copy(v2_s[:], tab2_s[:].indirect(offs2_sb[:]))
         gather_words(1)
+        order = [(b, half, t) for b in range(2) for half in range(2) for t in range(PACK)]
+        for key in order[:SPELL_BANKS]:
+            open_spell(key)
+        for key in order[:LATE_BANKS]:
+            open_resid(key)
         first_stage(0, 0)
         quantize_w1(1, 0)
         quantize_w1(1, 1)
         deal_w4(1)
         first_stage(0, 1)
         first_stage(1, 0)
-        first_stage(1, 1)
         quantize_h(0, 0)
         quantize_h(1, 0)
         for a in range(2):
             nc.vector.tensor_copy(v2_w[a][:], tab2_w[a][:].indirect(offs2_sb[:]))
-        nc.vector.tensor_scalar(
-            out=neg_temp[:], in0=temp_sb[:], scalar1=-1.0, scalar2=None, op0=ALU.mult
-        )
+        first_stage(1, 1)
         quantize_h(0, 1)
         quantize_h(1, 1)
         for half in range(2):

@@ -21,7 +21,7 @@ PASS = P * PACK
 HALF = 512
 LIST = 16
 
-CAST_VECTOR_SLOTS = {(0, 0): 0, (0, 1): 0, (1, 0): 4, (1, 1): 0}
+CAST_VECTOR_PAIRS = {(0, 0): 0, (0, 1): 0, (1, 0): 1, (1, 1): 1}
 SPELL_BANKS, LATE_BANKS = 3, 5
 WEAVE_PIECE = 256
 WEAVE_VECTOR_PIECES = {(0, 0): 0, (0, 1): 0, (1, 0): 1, (1, 1): 1}
@@ -58,6 +58,8 @@ def tile_list_surname_variant_looks_kernel(
 
         v_s = held([P, S], U8, "v_s")
         v2_s = held([P, S2], U8, "v2_s")
+        v_spread = held([P, S], U8, "v_spread")
+        v2_spread = held([P, S2], U8, "v2_spread")
         for plane in (tab_s, w4_raw_s, tab2_s, v_s, v2_s):
             nc.vector.memset(plane[:].bitcast(I32), 0)
 
@@ -70,7 +72,7 @@ def tile_list_surname_variant_looks_kernel(
 
         def close_up_scales(plane, spread):
             for q in range(4):
-                nc.gpsimd.dma_start(
+                nc.sync.dma_start(
                     out=plane[32 * q : 32 * q + 8, :].bitcast(I32),
                     in_=spread[32 * q : 32 * q + 32 : 4, :].bitcast(I32),
                 )
@@ -92,26 +94,30 @@ def tile_list_surname_variant_looks_kernel(
                 out=w4_raw[b][:], in_=words[:, :, b * PASS * 4 : (b + 1) * PASS * 4].bitcast(I32)
             )
 
-        for q in range(4):
-            nc.gpsimd.dma_start(
-                out=w4_raw_s[32 * q : 32 * q + 8, :].bitcast(I32),
-                in_=w4_scales[:, 4 * q : 4 * q + 4, :].bitcast(I32),
-            )
         nc.sync.dma_start(offs_sb[:], offs)
         load_w1(0, 0)
         load_spread_scales(tab_s, tab_scales)
         nc.sync.dma_start(offs2_sb[:], offs2)
         load_w1(0, 1)
         load_spread_scales(tab2_s, tab2_scales)
+        nc.vector.tensor_copy(v_spread[:], tab_s[:].indirect(offs_sb[:]))
+        nc.vector.tensor_copy(v2_spread[:], tab2_s[:].indirect(offs2_sb[:]))
         load_words(tab_w[0], tab_words, 0)
+        for q in range(4):
+            nc.sync.dma_start(
+                out=w4_raw_s[32 * q : 32 * q + 8, :].bitcast(I32),
+                in_=w4_scales[:, 4 * q : 4 * q + 4, :].bitcast(I32),
+            )
         load_words(tab_w[1], tab_words, 1, 0, T // 2)
         load_w4(0)
+        close_up_scales(v_s, v_spread)
         load_words(tab_w[1], tab_words, 1, T // 2, T)
         nc.sync.dma_start(out=gain_sb[:], in_=gain.rearrange("(b p t) -> p b t", b=2, t=PACK))
         load_w1(1, 0)
         load_w1(1, 1)
         load_w4(1)
         load_words(tab2_w[0], tab2_words, 0)
+        close_up_scales(v2_s, v2_spread)
         load_words(tab2_w[1], tab2_words, 1)
         nc.sync.dma_start(pos1_sb[:], pos1)
         nc.sync.dma_start(pos2_sb[:], pos2)
@@ -123,9 +129,7 @@ def tile_list_surname_variant_looks_kernel(
             return offs_sb[:, half * HALF // LIST : (half + 1) * HALF // LIST]
 
         v_w = {(a, half): held([P, HALF], U32, f"v_w{a}{half}") for a in range(2) for half in range(2)}
-        v_spread = held([P, S], U8, "v_spread")
         v2_w = [held([P, S2], U32, f"v2_w{a}") for a in range(2)]
-        v2_spread = held([P, S2], U8, "v2_spread")
 
         w4_s = held([P, H], U8, "w4_s")
 
@@ -147,11 +151,12 @@ def tile_list_surname_variant_looks_kernel(
             grouped = ring.tile([P, PASS * PACK], BF16, name="w1_grouped", align_bytes=64)
             dst = grouped[:].rearrange("p (t m j) -> p m j t", t=PACK, j=PACK)
             src = w1_raw[b, a][:].rearrange("p j (m t) -> p m j t", t=PACK)
-            cut = PACK - CAST_VECTOR_SLOTS[b, a]
-            if cut > 0:
-                nc.scalar.copy(out=dst[:, :, :, :cut], in_=src[:, :, :, :cut])
-            if cut < PACK:
-                nc.vector.tensor_copy(out=dst[:, :, :, cut:], in_=src[:, :, :, cut:])
+            for pair in range(2):
+                slots = slice(2 * pair, 2 * pair + 2)
+                if pair < 2 - CAST_VECTOR_PAIRS[b, a]:
+                    nc.scalar.copy(out=dst[:, :, :, slots], in_=src[:, :, :, slots])
+                else:
+                    nc.vector.tensor_copy(out=dst[:, :, :, slots], in_=src[:, :, :, slots])
             nc.vector.quantize_mx(out=w1_q[b, a][:].bitcast(FP8X4), scales=w1_s[b, a][:], in_=grouped[:])
 
         def deal_w4(b):
@@ -271,12 +276,8 @@ def tile_list_surname_variant_looks_kernel(
                 nc.scalar.activation(out=result[:], in_=weighted[:], func=ACT.Abs, bias=fam_sb[:, c : c + 1])
                 nc.sync.dma_start(out=out[c * P : (c + 1) * P, cols], in_=result[:])
 
-        nc.vector.tensor_copy(v_spread[:], tab_s[:].indirect(offs_sb[:]))
-        close_up_scales(v_s, v_spread)
         quantize_w1(0, 0)
         quantize_w1(0, 1)
-        nc.vector.tensor_copy(v2_spread[:], tab2_s[:].indirect(offs2_sb[:]))
-        close_up_scales(v2_s, v2_spread)
         gather_words(0)
         deal_w4_scales()
         deal_w4(0)

@@ -22,7 +22,8 @@ HALF = 512
 LIST = 16
 
 CAST_VECTOR_PAIRS = {(0, 0): 0, (0, 1): 0, (1, 0): 1, (1, 1): 1}
-SPELL_BANKS, LATE_BANKS = 3, 5
+SPELL_BANKS, LATE_BANKS = 4, 4
+QUADRANTS = (0, 2, 1, 3)
 WEAVE_PIECE = 256
 WEAVE_VECTOR_PIECES = {(0, 0): 0, (0, 1): 0, (1, 0): 1, (1, 1): 1}
 
@@ -64,14 +65,14 @@ def tile_list_surname_variant_looks_kernel(
             nc.vector.memset(plane[:].bitcast(I32), 0)
 
         def load_spread_scales(window, scales):
-            for q in range(4):
+            for q in QUADRANTS:
                 nc.sync.dma_start(
                     out=window[32 * q : 32 * q + 32 : 4, :].bitcast(I32),
                     in_=scales[:, 4 * q : 4 * q + 4, :].bitcast(I32),
                 )
 
         def close_up_scales(plane, spread):
-            for q in range(4):
+            for q in QUADRANTS:
                 nc.sync.dma_start(
                     out=plane[32 * q : 32 * q + 8, :].bitcast(I32),
                     in_=spread[32 * q : 32 * q + 32 : 4, :].bitcast(I32),
@@ -94,8 +95,8 @@ def tile_list_surname_variant_looks_kernel(
                 out=w4_raw[b][:], in_=words[:, :, b * PASS * 4 : (b + 1) * PASS * 4].bitcast(I32)
             )
 
-        nc.sync.dma_start(offs_sb[:], offs)
         load_w1(0, 0)
+        nc.sync.dma_start(offs_sb[:], offs)
         load_spread_scales(tab_s, tab_scales)
         nc.sync.dma_start(offs2_sb[:], offs2)
         load_w1(0, 1)
@@ -103,7 +104,7 @@ def tile_list_surname_variant_looks_kernel(
         nc.vector.tensor_copy(v_spread[:], tab_s[:].indirect(offs_sb[:]))
         nc.vector.tensor_copy(v2_spread[:], tab2_s[:].indirect(offs2_sb[:]))
         load_words(tab_w[0], tab_words, 0)
-        for q in range(4):
+        for q in QUADRANTS:
             nc.sync.dma_start(
                 out=w4_raw_s[32 * q : 32 * q + 8, :].bitcast(I32),
                 in_=w4_scales[:, 4 * q : 4 * q + 4, :].bitcast(I32),
@@ -293,11 +294,11 @@ def tile_list_surname_variant_looks_kernel(
         deal_w4(1)
         first_stage(0, 1)
         first_stage(1, 0)
+        first_stage(1, 1)
         quantize_h(0, 0)
         quantize_h(1, 0)
         for a in range(2):
             nc.vector.tensor_copy(v2_w[a][:], tab2_w[a][:].indirect(offs2_sb[:]))
-        first_stage(1, 1)
         quantize_h(0, 1)
         quantize_h(1, 1)
         for half in range(2):

@@ -18,14 +18,15 @@ ALU = mybir.AluOpType
 P = 128
 PACK = 4
 PASS = P * PACK
+PASSES = K // PASS
 HALF = 512
+HALVES = S // HALF
+FAMILY_TILES = S2 // P
 LIST = 16
-
-CAST_VECTOR_PAIRS = {(0, 0): 0, (0, 1): 0, (1, 0): 1, (1, 1): 1}
+QUADRANT = 32
+RUN = 4
 SPELL_BANKS, LATE_BANKS = 4, 4
 QUADRANTS = (0, 2, 1, 3)
-WEAVE_PIECE = 256
-WEAVE_VECTOR_PIECES = {(0, 0): 0, (0, 1): 0, (1, 0): 1, (1, 1): 1}
 
 
 def tile_list_surname_variant_looks_kernel(
@@ -45,44 +46,45 @@ def tile_list_surname_variant_looks_kernel(
         offs2_sb = keep.tile([P, S2 // LIST], U16, name="offs2_sb")
         pos1_sb = keep.tile([P, NP // LIST], U16, name="pos1_sb")
         pos2_sb = keep.tile([P, NP // LIST], U16, name="pos2_sb")
-        gain_sb = held([P, 2, PACK], F32, "gain_sb")
-        temp_sb = held([P, 4], F32, "temp_sb")
-        fam_sb = held([P, 4], F32, "fam_sb")
+        gain_sb = held([P, PASSES, PACK], F32, "gain_sb")
+        temp_sb = held([P, FAMILY_TILES], F32, "temp_sb")
+        fam_sb = held([P, FAMILY_TILES], F32, "fam_sb")
 
-        tab_w = [held([P, T], U32, f"tab_w{a}") for a in range(2)]
+        tab_w = [held([P, T], U32, f"tab_w{a}") for a in range(PASSES)]
         tab_s = held([P, T], U8, "tab_s")
-        tab2_w = [held([P, T3], U32, f"tab2_w{a}") for a in range(2)]
+        tab2_w = [held([P, T3], U32, f"tab2_w{b}") for b in range(PASSES)]
         tab2_s = held([P, T3], U8, "tab2_s")
-        w4_raw = [held([P, 2, PASS], I32, f"w4_raw{b}") for b in range(2)]
+        w4_raw = [held([P, PASSES, PASS], I32, f"w4_raw{b}") for b in range(PASSES)]
         w4_raw_s = held([P, H], U8, "w4_raw_s")
-        w1_raw = {(b, a): held([P, PACK, PASS], F32, f"w1_raw{b}{a}") for b in range(2) for a in range(2)}
+        w1_raw = {
+            (b, a): held([P, PACK, PASS], F32, f"w1_raw{b}{a}") for b in range(PASSES) for a in range(PASSES)
+        }
 
         v_s = held([P, S], U8, "v_s")
         v2_s = held([P, S2], U8, "v2_s")
         v_spread = held([P, S], U8, "v_spread")
         v2_spread = held([P, S2], U8, "v2_spread")
-        for plane in (tab_s, w4_raw_s, tab2_s, v_s, v2_s):
-            nc.vector.memset(plane[:].bitcast(I32), 0)
+        for tile in (tab_s, w4_raw_s, tab2_s, v_s, v2_s):
+            nc.vector.memset(tile[:].bitcast(I32), 0)
 
-        def load_spread_scales(window, scales):
+        def spread_rows(tile, q):
+            return tile[QUADRANT * q : QUADRANT * (q + 1) : 4, :].bitcast(I32)
+
+        def plane_rows(tile, q):
+            return tile[QUADRANT * q : QUADRANT * q + 4 * PASSES, :].bitcast(I32)
+
+        def load_scales(rows, tile, scales):
             for q in QUADRANTS:
-                nc.sync.dma_start(
-                    out=window[32 * q : 32 * q + 32 : 4, :].bitcast(I32),
-                    in_=scales[:, 4 * q : 4 * q + 4, :].bitcast(I32),
-                )
+                nc.sync.dma_start(out=rows(tile, q), in_=scales[:, 4 * q : 4 * q + 4, :].bitcast(I32))
 
         def close_up_scales(plane, spread):
             for q in QUADRANTS:
-                nc.sync.dma_start(
-                    out=plane[32 * q : 32 * q + 8, :].bitcast(I32),
-                    in_=spread[32 * q : 32 * q + 32 : 4, :].bitcast(I32),
-                )
+                nc.sync.dma_start(out=plane_rows(plane, q), in_=spread_rows(spread, q))
 
-        def load_words(tile, words, a, first=0, last=None):
-            last = tile.shape[1] if last is None else last
+        def load_words(tile, words, first, last):
             nc.sync.dma_start(
                 out=tile[:, first:last].bitcast(I32),
-                in_=words[a, :, first:last].rearrange("p t i -> p (t i)").bitcast(I32),
+                in_=words[:, first:last].rearrange("p t i -> p (t i)").bitcast(I32),
             )
 
         def load_w1(b, a):
@@ -92,92 +94,84 @@ def tile_list_surname_variant_looks_kernel(
         def load_w4(b):
             words = w4_words.rearrange("a p c i -> p a (c i)")
             nc.sync.dma_start(
-                out=w4_raw[b][:], in_=words[:, :, b * PASS * 4 : (b + 1) * PASS * 4].bitcast(I32)
+                out=w4_raw[b][:], in_=words[:, :, b * PASS * PACK : (b + 1) * PASS * PACK].bitcast(I32)
             )
 
         load_w1(0, 0)
         nc.sync.dma_start(offs_sb[:], offs)
-        load_spread_scales(tab_s, tab_scales)
+        load_scales(spread_rows, tab_s, tab_scales)
         nc.sync.dma_start(offs2_sb[:], offs2)
         load_w1(0, 1)
-        load_spread_scales(tab2_s, tab2_scales)
+        load_scales(spread_rows, tab2_s, tab2_scales)
         nc.vector.tensor_copy(v_spread[:], tab_s[:].indirect(offs_sb[:]))
         nc.vector.tensor_copy(v2_spread[:], tab2_s[:].indirect(offs2_sb[:]))
-        load_words(tab_w[0], tab_words, 0)
-        for q in QUADRANTS:
-            nc.sync.dma_start(
-                out=w4_raw_s[32 * q : 32 * q + 8, :].bitcast(I32),
-                in_=w4_scales[:, 4 * q : 4 * q + 4, :].bitcast(I32),
-            )
-        load_words(tab_w[1], tab_words, 1, 0, T // 2)
+        load_words(tab_w[0], tab_words[0], 0, T)
+        load_scales(plane_rows, w4_raw_s, w4_scales)
+        load_words(tab_w[1], tab_words[1], 0, T // 2)
         load_w4(0)
         close_up_scales(v_s, v_spread)
-        load_words(tab_w[1], tab_words, 1, T // 2, T)
-        nc.sync.dma_start(out=gain_sb[:], in_=gain.rearrange("(b p t) -> p b t", b=2, t=PACK))
+        load_words(tab_w[1], tab_words[1], T // 2, T)
+        nc.sync.dma_start(out=gain_sb[:], in_=gain.rearrange("(b p t) -> p b t", b=PASSES, t=PACK))
         load_w1(1, 0)
         load_w1(1, 1)
         load_w4(1)
-        load_words(tab2_w[0], tab2_words, 0)
+        load_words(tab2_w[0], tab2_words[0], 0, T3)
         close_up_scales(v2_s, v2_spread)
-        load_words(tab2_w[1], tab2_words, 1)
+        load_words(tab2_w[1], tab2_words[1], 0, T3)
         nc.sync.dma_start(pos1_sb[:], pos1)
         nc.sync.dma_start(pos2_sb[:], pos2)
         with nc.allow_non_contiguous_dma(reason="one value a partition"):
             nc.sync.dma_start(out=temp_sb[:], in_=temp.rearrange("(c p) -> p c", p=P))
             nc.sync.dma_start(out=fam_sb[:], in_=fam.rearrange("(c p) -> p c", p=P))
 
-        def entries(half):
-            return offs_sb[:, half * HALF // LIST : (half + 1) * HALF // LIST]
-
-        v_w = {(a, half): held([P, HALF], U32, f"v_w{a}{half}") for a in range(2) for half in range(2)}
-        v2_w = [held([P, S2], U32, f"v2_w{a}") for a in range(2)]
-
+        v_w = {
+            (a, half): held([P, HALF], U32, f"v_w{a}{half}") for a in range(PASSES) for half in range(HALVES)
+        }
+        v2_w = [held([P, S2], U32, f"v2_w{b}") for b in range(PASSES)]
         w4_s = held([P, H], U8, "w4_s")
+        w1_q = {key: held([P, PASS], U32, f"w1_q{key[0]}{key[1]}") for key in w1_raw}
+        w1_s = {key: held([P, PASS], U8, f"w1_s{key[0]}{key[1]}") for key in w1_raw}
+        w4_q = [held([P, PASSES, PASS], I32, f"w4_q{b}") for b in range(PASSES)]
 
         def gather_words(a):
-            for half in range(2):
-                nc.vector.tensor_copy(v_w[a, half][:], tab_w[a][:].indirect(entries(half)))
+            for half in range(HALVES):
+                entries = offs_sb[:, half * HALF // LIST : (half + 1) * HALF // LIST]
+                nc.vector.tensor_copy(v_w[a, half][:], tab_w[a][:].indirect(entries))
 
         def deal_w4_scales():
             nc.vector.tensor_copy(
-                out=w4_s[:].rearrange("p (b t m) -> p b t m", b=2, t=PACK),
-                in_=w4_raw_s[:].rearrange("p (b m t) -> p b t m", b=2, t=PACK),
+                out=w4_s[:].rearrange("p (b t m) -> p b t m", b=PASSES, t=PACK),
+                in_=w4_raw_s[:].rearrange("p (b m t) -> p b t m", b=PASSES, t=PACK),
             )
 
-        w1_q = {key: held([P, PASS], U32, f"w1_q{key[0]}{key[1]}") for key in w1_raw}
-        w1_s = {key: held([P, PASS], U8, f"w1_s{key[0]}{key[1]}") for key in w1_raw}
-        w4_q = [held([P, 2, PASS], I32, f"w4_q{b}") for b in range(2)]
+        def deal_w4(b):
+            nc.vector.tensor_copy(
+                out=w4_q[b][:].rearrange("p a (t c i) -> p a c t i", t=PACK, i=RUN),
+                in_=w4_raw[b][:].rearrange("p a (c i t) -> p a c t i", t=PACK, i=RUN),
+            )
 
         def quantize_w1(b, a):
             grouped = ring.tile([P, PASS * PACK], BF16, name="w1_grouped", align_bytes=64)
             dst = grouped[:].rearrange("p (t m j) -> p m j t", t=PACK, j=PACK)
             src = w1_raw[b, a][:].rearrange("p j (m t) -> p m j t", t=PACK)
-            for pair in range(2):
-                slots = slice(2 * pair, 2 * pair + 2)
-                if pair < 2 - CAST_VECTOR_PAIRS[b, a]:
-                    nc.scalar.copy(out=dst[:, :, :, slots], in_=src[:, :, :, slots])
-                else:
-                    nc.vector.tensor_copy(out=dst[:, :, :, slots], in_=src[:, :, :, slots])
+            second_copy = nc.scalar.copy if b == 0 else nc.vector.tensor_copy
+            nc.scalar.copy(out=dst[:, :, :, :2], in_=src[:, :, :, :2])
+            second_copy(out=dst[:, :, :, 2:], in_=src[:, :, :, 2:])
             nc.vector.quantize_mx(out=w1_q[b, a][:].bitcast(FP8X4), scales=w1_s[b, a][:], in_=grouped[:])
 
-        def deal_w4(b):
-            nc.vector.tensor_copy(
-                out=w4_q[b][:].rearrange("p a (t c i) -> p a c t i", t=PACK, i=4),
-                in_=w4_raw[b][:].rearrange("p a (c i t) -> p a c t i", t=PACK, i=4),
-            )
-
         h_rows = {}
-        h_q = {(b, half): held([P, HALF], U32, f"h_q{b}{half}") for b in range(2) for half in range(2)}
-        h_s = {(b, half): held([P, HALF], U8, f"h_s{b}{half}") for b in range(2) for half in range(2)}
+        h_keys = [(b, half) for b in range(PASSES) for half in range(HALVES)]
+        h_q = {(b, half): held([P, HALF], U32, f"h_q{b}{half}") for b, half in h_keys}
+        h_s = {(b, half): held([P, HALF], U8, f"h_s{b}{half}") for b, half in h_keys}
 
         def spell_pass(bank, b, half, t, a):
-            cols = slice(t * P, (t + 1) * P)
+            places = slice(t * P, (t + 1) * P)
             nc.tensor.matmul_mx(
                 out=bank[:],
-                lhsT=w1_q[b, a][:, cols].bitcast(FP8X4), lhsT_scale=w1_s[b, a][:, cols],
+                lhsT=w1_q[b, a][:, places].bitcast(FP8X4), lhsT_scale=w1_s[b, a][:, places],
                 rhs=v_w[a, half][:].bitcast(FP8X4),
                 rhs_scale=v_s[4 * a :, half * HALF : (half + 1) * HALF],
-                start=(a == 0), stop=(a == 1),
+                start=(a == 0), stop=(a == PASSES - 1),
             )
 
         def resid_pass(bank, b, half, t, a):
@@ -187,7 +181,7 @@ def tile_list_surname_variant_looks_kernel(
                 lhsT_scale=w4_s[4 * a :, b * PASS + t * P : b * PASS + (t + 1) * P],
                 rhs=v_w[a, half][:].bitcast(FP8X4),
                 rhs_scale=v_s[4 * a :, half * HALF : (half + 1) * HALF],
-                start=(a == 0), stop=(a == 1),
+                start=(a == 0), stop=(a == PASSES - 1),
             )
 
         spell_open, resid_open = {}, {}
@@ -201,64 +195,59 @@ def tile_list_surname_variant_looks_kernel(
             resid_pass(resid_open[key], *key, 0)
 
         def first_stage(b, half):
-            rows = ring.tile([P, PACK, HALF], BF16, name="h_rows", bufs=4, align_bytes=64)
+            rows = ring.tile([P, PACK, HALF], BF16, name="h_rows", bufs=len(h_keys), align_bytes=64)
             h_rows[b, half] = rows
             for t in range(PACK):
                 key = (b, half, t)
                 if key not in spell_open:
                     open_spell(key)
-                spell = spell_open[key]
-                spell_pass(spell, *key, 1)
+                spell_pass(spell_open[key], *key, 1)
                 if key not in resid_open:
                     open_resid(key)
-                resid = resid_open[key]
-                resid_pass(resid, *key, 1)
-                bent = ring.tile([P, HALF], F32, name="bent", bufs=3)
-                nc.scalar.activation(out=bent[:], in_=spell[:], func=ACT.Tanh)
+                resid_pass(resid_open[key], *key, 1)
+                bent = ring.tile([P, HALF], F32, name="bent", bufs=SPELL_BANKS)
+                nc.scalar.activation(out=bent[:], in_=spell_open[key][:], func=ACT.Tanh)
                 nc.vector.scalar_tensor_tensor(
-                    out=rows[:, t, :], in0=bent[:], scalar=gain_sb[:, b, t : t + 1], in1=resid[:],
+                    out=rows[:, t, :], in0=bent[:], scalar=gain_sb[:, b, t : t + 1], in1=resid_open[key][:],
                     op0=ALU.mult, op1=ALU.add,
                 )
 
         def quantize_h(b, half):
-            woven = ring.tile([P, HALF * PACK], BF16, name="woven", align_bytes=64)
-            dst = woven[:].rearrange("p (c i t) -> p c t i", t=PACK, i=4)
-            src = h_rows[b, half][:].rearrange("p t (c i) -> p c t i", i=4)
-            pieces = HALF // WEAVE_PIECE
-            for piece in range(pieces):
-                cols = slice(piece * WEAVE_PIECE // 4, (piece + 1) * WEAVE_PIECE // 4)
-                if piece < pieces - WEAVE_VECTOR_PIECES[b, half]:
-                    nc.scalar.copy(out=dst[:, cols], in_=src[:, cols])
-                else:
-                    nc.vector.tensor_copy(out=dst[:, cols], in_=src[:, cols])
+            woven = ring.tile([P, HALF * PACK], BF16, name="woven", bufs=3, align_bytes=64)
+            dst = woven[:].rearrange("p (c i t) -> p c t i", t=PACK, i=RUN)
+            src = h_rows[b, half][:].rearrange("p t (c i) -> p c t i", i=RUN)
+            middle = HALF // RUN // 2
+            second_copy = nc.vector.tensor_copy if (b, half) == h_keys[-1] else nc.scalar.copy
+            nc.scalar.copy(out=dst[:, :middle], in_=src[:, :middle])
+            second_copy(out=dst[:, middle:], in_=src[:, middle:])
             nc.vector.quantize_mx(out=h_q[b, half][:].bitcast(FP8X4), scales=h_s[b, half][:], in_=woven[:])
 
-        scores = [held([P, S], F32, f"scores{c}") for c in range(4)]
-        top = held([P, 4, 2], F32, "top")
-        bias = held([P, 4], F32, "bias")
+        scores = [held([P, S], F32, f"scores{c}") for c in range(FAMILY_TILES)]
+        top = held([P, FAMILY_TILES, HALVES], F32, "top")
+        bias = held([P, FAMILY_TILES], F32, "bias")
 
         def second_stage(c, half):
-            cols = slice(c * P, (c + 1) * P)
+            names = slice(c * P, (c + 1) * P)
             score = psum.tile([P, HALF], F32, name="score", tag="late", bufs=LATE_BANKS)
-            for b in range(2):
+            for b in range(PASSES):
                 nc.tensor.matmul_mx(
                     out=score[:],
-                    lhsT=v2_w[b][:, cols].bitcast(FP8X4), lhsT_scale=v2_s[4 * b :, cols],
+                    lhsT=v2_w[b][:, names].bitcast(FP8X4), lhsT_scale=v2_s[4 * b :, names],
                     rhs=h_q[b, half][:].bitcast(FP8X4), rhs_scale=h_s[b, half][:],
-                    start=(b == 0), stop=(b == 1),
+                    start=(b == 0), stop=(b == PASSES - 1),
                 )
             nc.vector.tensor_scalar(
                 out=scores[c][:, half * HALF : (half + 1) * HALF], in0=score[:],
-                scalar1=1.0, scalar2=(top[:, c, 0:1] if half == 1 else None),
+                scalar1=1.0, scalar2=(top[:, c, half - 1 : half] if half > 0 else None),
                 op0=ALU.mult, op1=ALU.max, accum_out=top[:, c, half : half + 1],
             )
 
-        def looks(c):
+        def latin_look(c):
             nc.gpsimd.tensor_scalar(
-                out=bias[:, c : c + 1], in0=top[:, c, 1:2], scalar1=temp_sb[:, c : c + 1], scalar2=-1.0,
-                op0=ALU.mult, op1=ALU.mult,
+                out=bias[:, c : c + 1], in0=top[:, c, HALVES - 1 : HALVES],
+                scalar1=temp_sb[:, c : c + 1], scalar2=-1.0, op0=ALU.mult, op1=ALU.mult,
             )
-            latin = ring.tile([P, NP], F32, name="latin", bufs=4)
+            latin = ring.tile([P, NP], F32, name="latin", bufs=FAMILY_TILES)
             nc.scalar.activation(
                 out=latin[:], in_=scores[c][:].indirect(pos1_sb[:]), func=ACT.Exp,
                 bias=bias[:, c : c + 1], scale=temp_sb[:, c : c + 1],
@@ -266,44 +255,43 @@ def tile_list_surname_variant_looks_kernel(
             return latin
 
         def finish(c, latin):
-            pieces = 2 if c == 3 else 1
+            pieces = 2 if c == FAMILY_TILES - 1 else 1
             width = NP // pieces
             for piece in range(pieces):
                 cols = slice(piece * width, (piece + 1) * width)
                 picks = pos2_sb[:, piece * width // LIST : (piece + 1) * width // LIST]
-                weighted = ring.tile([P, width], F32, name="weighted", bufs=4)
+                weighted = ring.tile([P, width], F32, name="weighted", bufs=FAMILY_TILES)
                 nc.vector.tensor_tensor(weighted[:], scores[c][:].indirect(picks), latin[:, cols], ALU.mult)
-                result = ring.tile([P, width], F32, name="result", bufs=5)
+                result = ring.tile([P, width], F32, name="result", bufs=FAMILY_TILES + 1)
                 nc.scalar.activation(out=result[:], in_=weighted[:], func=ACT.Abs, bias=fam_sb[:, c : c + 1])
                 nc.sync.dma_start(out=out[c * P : (c + 1) * P, cols], in_=result[:])
 
-        quantize_w1(0, 0)
-        quantize_w1(0, 1)
+        for a in range(PASSES):
+            quantize_w1(0, a)
         gather_words(0)
         deal_w4_scales()
         deal_w4(0)
         gather_words(1)
-        order = [(b, half, t) for b in range(2) for half in range(2) for t in range(PACK)]
-        for key in order[:SPELL_BANKS]:
+        slots = [(b, half, t) for b, half in h_keys for t in range(PACK)]
+        for key in slots[:SPELL_BANKS]:
             open_spell(key)
-        for key in order[:LATE_BANKS]:
+        for key in slots[:LATE_BANKS]:
             open_resid(key)
-        first_stage(0, 0)
-        quantize_w1(1, 0)
-        quantize_w1(1, 1)
+        first_stage(*h_keys[0])
+        for a in range(PASSES):
+            quantize_w1(1, a)
         deal_w4(1)
-        first_stage(0, 1)
-        first_stage(1, 0)
-        first_stage(1, 1)
-        quantize_h(0, 0)
-        quantize_h(1, 0)
-        for a in range(2):
-            nc.vector.tensor_copy(v2_w[a][:], tab2_w[a][:].indirect(offs2_sb[:]))
-        quantize_h(0, 1)
-        quantize_h(1, 1)
-        for half in range(2):
-            for c in range(4):
+        for key in h_keys[1:]:
+            first_stage(*key)
+        for b in range(PASSES):
+            quantize_h(b, 0)
+        for b in range(PASSES):
+            nc.vector.tensor_copy(v2_w[b][:], tab2_w[b][:].indirect(offs2_sb[:]))
+        for b in range(PASSES):
+            quantize_h(b, 1)
+        for half in range(HALVES):
+            for c in range(FAMILY_TILES):
                 second_stage(c, half)
-        latins = [looks(c) for c in range(4)]
-        for c in range(4):
+        latins = [latin_look(c) for c in range(FAMILY_TILES)]
+        for c in range(FAMILY_TILES):
             finish(c, latins[c])

from contextlib import ExitStack

import concourse.mybir as mybir

K, H, T, S, S2, T3, NP = 1024, 1024, 4096, 1024, 512, 2048, 512
FLOPS = 2 * K * H * S * 2 + 2 * H * S2 * S

F32 = mybir.dt.float32
BF16 = mybir.dt.bfloat16
I32 = mybir.dt.int32
U32 = mybir.dt.uint32
U16 = mybir.dt.uint16
U8 = mybir.dt.uint8
FP8X4 = mybir.dt.float8_e4m3fn_x4
ACT = mybir.ActivationFunctionType
ALU = mybir.AluOpType

P = 128
PACK = 4
PASS = P * PACK
PASSES = K // PASS
HALF = 512
HALVES = S // HALF
FAMILY_TILES = S2 // P
LIST = 16
QUADRANT = 32
RUN = 4
SPELL_BANKS, LATE_BANKS = 4, 4
QUADRANTS = (0, 2, 1, 3)


def tile_list_surname_variant_looks_kernel(
    tc, tab_words, tab_scales, offs, tab2_words, tab2_scales, offs2, pos1, pos2,
    w1, w4_words, w4_scales, gain, temp, fam, out,
):
    nc = tc.nc
    with ExitStack() as ctx:
        keep = ctx.enter_context(tc.tile_pool(name="keep", bufs=1))
        ring = ctx.enter_context(tc.tile_pool(name="ring", bufs=2))
        psum = ctx.enter_context(tc.psum_pool(name="psum", bufs=1))

        def held(shape, dtype, name):
            return keep.tile(shape, dtype, name=name, align_bytes=64)

        offs_sb = keep.tile([P, S // LIST], U16, name="offs_sb")
        offs2_sb = keep.tile([P, S2 // LIST], U16, name="offs2_sb")
        pos1_sb = keep.tile([P, NP // LIST], U16, name="pos1_sb")
        pos2_sb = keep.tile([P, NP // LIST], U16, name="pos2_sb")
        gain_sb = held([P, PASSES, PACK], F32, "gain_sb")
        temp_sb = held([P, FAMILY_TILES], F32, "temp_sb")
        fam_sb = held([P, FAMILY_TILES], F32, "fam_sb")

        tab_w = [held([P, T], U32, f"tab_w{a}") for a in range(PASSES)]
        tab_s = held([P, T], U8, "tab_s")
        tab2_w = [held([P, T3], U32, f"tab2_w{b}") for b in range(PASSES)]
        tab2_s = held([P, T3], U8, "tab2_s")
        w4_raw = [held([P, PASSES, PASS], I32, f"w4_raw{b}") for b in range(PASSES)]
        w4_raw_s = held([P, H], U8, "w4_raw_s")
        w1_raw = {
            (b, a): held([P, PACK, PASS], F32, f"w1_raw{b}{a}") for b in range(PASSES) for a in range(PASSES)
        }

        v_s = held([P, S], U8, "v_s")
        v2_s = held([P, S2], U8, "v2_s")
        v_spread = held([P, S], U8, "v_spread")
        v2_spread = held([P, S2], U8, "v2_spread")
        for tile in (tab_s, w4_raw_s, tab2_s, v_s, v2_s):
            nc.vector.memset(tile[:].bitcast(I32), 0)

        def spread_rows(tile, q):
            return tile[QUADRANT * q : QUADRANT * (q + 1) : 4, :].bitcast(I32)

        def plane_rows(tile, q):
            return tile[QUADRANT * q : QUADRANT * q + 4 * PASSES, :].bitcast(I32)

        def load_scales(rows, tile, scales):
            for q in QUADRANTS:
                nc.sync.dma_start(out=rows(tile, q), in_=scales[:, 4 * q : 4 * q + 4, :].bitcast(I32))

        def close_up_scales(plane, spread):
            for q in QUADRANTS:
                nc.sync.dma_start(out=plane_rows(plane, q), in_=spread_rows(spread, q))

        def load_words(tile, words, first, last):
            nc.sync.dma_start(
                out=tile[:, first:last].bitcast(I32),
                in_=words[:, first:last].rearrange("p t i -> p (t i)").bitcast(I32),
            )

        def load_w1(b, a):
            rows = w1[a * PASS : (a + 1) * PASS, b * PASS : (b + 1) * PASS]
            nc.sync.dma_start(out=w1_raw[b, a][:], in_=rows.rearrange("(p j) c -> p j c", j=PACK))

        def load_w4(b):
            words = w4_words.rearrange("a p c i -> p a (c i)")
            nc.sync.dma_start(
                out=w4_raw[b][:], in_=words[:, :, b * PASS * PACK : (b + 1) * PASS * PACK].bitcast(I32)
            )

        load_w1(0, 0)
        nc.sync.dma_start(offs_sb[:], offs)
        load_scales(spread_rows, tab_s, tab_scales)
        nc.sync.dma_start(offs2_sb[:], offs2)
        load_w1(0, 1)
        load_scales(spread_rows, tab2_s, tab2_scales)
        nc.vector.tensor_copy(v_spread[:], tab_s[:].indirect(offs_sb[:]))
        nc.vector.tensor_copy(v2_spread[:], tab2_s[:].indirect(offs2_sb[:]))
        load_words(tab_w[0], tab_words[0], 0, T)
        load_scales(plane_rows, w4_raw_s, w4_scales)
        load_words(tab_w[1], tab_words[1], 0, T // 2)
        load_w4(0)
        close_up_scales(v_s, v_spread)
        load_words(tab_w[1], tab_words[1], T // 2, T)
        nc.sync.dma_start(out=gain_sb[:], in_=gain.rearrange("(b p t) -> p b t", b=PASSES, t=PACK))
        load_w1(1, 0)
        load_w1(1, 1)
        load_w4(1)
        load_words(tab2_w[0], tab2_words[0], 0, T3)
        close_up_scales(v2_s, v2_spread)
        load_words(tab2_w[1], tab2_words[1], 0, T3)
        nc.sync.dma_start(pos1_sb[:], pos1)
        nc.sync.dma_start(pos2_sb[:], pos2)
        with nc.allow_non_contiguous_dma(reason="one value a partition"):
            nc.sync.dma_start(out=temp_sb[:], in_=temp.rearrange("(c p) -> p c", p=P))
            nc.sync.dma_start(out=fam_sb[:], in_=fam.rearrange("(c p) -> p c", p=P))

        v_w = {
            (a, half): held([P, HALF], U32, f"v_w{a}{half}") for a in range(PASSES) for half in range(HALVES)
        }
        v2_w = [held([P, S2], U32, f"v2_w{b}") for b in range(PASSES)]
        w4_s = held([P, H], U8, "w4_s")
        w1_q = {key: held([P, PASS], U32, f"w1_q{key[0]}{key[1]}") for key in w1_raw}
        w1_s = {key: held([P, PASS], U8, f"w1_s{key[0]}{key[1]}") for key in w1_raw}
        w4_q = [held([P, PASSES, PASS], I32, f"w4_q{b}") for b in range(PASSES)]

        def gather_words(a):
            for half in range(HALVES):
                entries = offs_sb[:, half * HALF // LIST : (half + 1) * HALF // LIST]
                nc.vector.tensor_copy(v_w[a, half][:], tab_w[a][:].indirect(entries))

        def deal_w4_scales():
            nc.vector.tensor_copy(
                out=w4_s[:].rearrange("p (b t m) -> p b t m", b=PASSES, t=PACK),
                in_=w4_raw_s[:].rearrange("p (b m t) -> p b t m", b=PASSES, t=PACK),
            )

        def deal_w4(b):
            nc.vector.tensor_copy(
                out=w4_q[b][:].rearrange("p a (t c i) -> p a c t i", t=PACK, i=RUN),
                in_=w4_raw[b][:].rearrange("p a (c i t) -> p a c t i", t=PACK, i=RUN),
            )

        def quantize_w1(b, a):
            grouped = ring.tile([P, PASS * PACK], BF16, name="w1_grouped", align_bytes=64)
            dst = grouped[:].rearrange("p (t m j) -> p m j t", t=PACK, j=PACK)
            src = w1_raw[b, a][:].rearrange("p j (m t) -> p m j t", t=PACK)
            second_copy = nc.scalar.copy if b == 0 else nc.vector.tensor_copy
            nc.scalar.copy(out=dst[:, :, :, :2], in_=src[:, :, :, :2])
            second_copy(out=dst[:, :, :, 2:], in_=src[:, :, :, 2:])
            nc.vector.quantize_mx(out=w1_q[b, a][:].bitcast(FP8X4), scales=w1_s[b, a][:], in_=grouped[:])

        h_rows = {}
        h_keys = [(b, half) for b in range(PASSES) for half in range(HALVES)]
        h_q = {(b, half): held([P, HALF], U32, f"h_q{b}{half}") for b, half in h_keys}
        h_s = {(b, half): held([P, HALF], U8, f"h_s{b}{half}") for b, half in h_keys}

        def spell_pass(bank, b, half, t, a):
            places = slice(t * P, (t + 1) * P)
            nc.tensor.matmul_mx(
                out=bank[:],
                lhsT=w1_q[b, a][:, places].bitcast(FP8X4), lhsT_scale=w1_s[b, a][:, places],
                rhs=v_w[a, half][:].bitcast(FP8X4),
                rhs_scale=v_s[4 * a :, half * HALF : (half + 1) * HALF],
                start=(a == 0), stop=(a == PASSES - 1),
            )

        def resid_pass(bank, b, half, t, a):
            nc.tensor.matmul_mx(
                out=bank[:],
                lhsT=w4_q[b][:, a, t * P : (t + 1) * P].bitcast(FP8X4),
                lhsT_scale=w4_s[4 * a :, b * PASS + t * P : b * PASS + (t + 1) * P],
                rhs=v_w[a, half][:].bitcast(FP8X4),
                rhs_scale=v_s[4 * a :, half * HALF : (half + 1) * HALF],
                start=(a == 0), stop=(a == PASSES - 1),
            )

        spell_open, resid_open = {}, {}

        def open_spell(key):
            spell_open[key] = psum.tile([P, HALF], F32, name="spell", bufs=SPELL_BANKS)
            spell_pass(spell_open[key], *key, 0)

        def open_resid(key):
            resid_open[key] = psum.tile([P, HALF], F32, name="resid", tag="late", bufs=LATE_BANKS)
            resid_pass(resid_open[key], *key, 0)

        def first_stage(b, half):
            rows = ring.tile([P, PACK, HALF], BF16, name="h_rows", bufs=len(h_keys), align_bytes=64)
            h_rows[b, half] = rows
            for t in range(PACK):
                key = (b, half, t)
                if key not in spell_open:
                    open_spell(key)
                spell_pass(spell_open[key], *key, 1)
                if key not in resid_open:
                    open_resid(key)
                resid_pass(resid_open[key], *key, 1)
                bent = ring.tile([P, HALF], F32, name="bent", bufs=SPELL_BANKS)
                nc.scalar.activation(out=bent[:], in_=spell_open[key][:], func=ACT.Tanh)
                nc.vector.scalar_tensor_tensor(
                    out=rows[:, t, :], in0=bent[:], scalar=gain_sb[:, b, t : t + 1], in1=resid_open[key][:],
                    op0=ALU.mult, op1=ALU.add,
                )

        def quantize_h(b, half):
            woven = ring.tile([P, HALF * PACK], BF16, name="woven", bufs=3, align_bytes=64)
            dst = woven[:].rearrange("p (c i t) -> p c t i", t=PACK, i=RUN)
            src = h_rows[b, half][:].rearrange("p t (c i) -> p c t i", i=RUN)
            middle = HALF // RUN // 2
            second_copy = nc.vector.tensor_copy if (b, half) == h_keys[-1] else nc.scalar.copy
            nc.scalar.copy(out=dst[:, :middle], in_=src[:, :middle])
            second_copy(out=dst[:, middle:], in_=src[:, middle:])
            nc.vector.quantize_mx(out=h_q[b, half][:].bitcast(FP8X4), scales=h_s[b, half][:], in_=woven[:])

        scores = [held([P, S], F32, f"scores{c}") for c in range(FAMILY_TILES)]
        top = held([P, FAMILY_TILES, HALVES], F32, "top")
        bias = held([P, FAMILY_TILES], F32, "bias")

        def second_stage(c, half):
            names = slice(c * P, (c + 1) * P)
            score = psum.tile([P, HALF], F32, name="score", tag="late", bufs=LATE_BANKS)
            for b in range(PASSES):
                nc.tensor.matmul_mx(
                    out=score[:],
                    lhsT=v2_w[b][:, names].bitcast(FP8X4), lhsT_scale=v2_s[4 * b :, names],
                    rhs=h_q[b, half][:].bitcast(FP8X4), rhs_scale=h_s[b, half][:],
                    start=(b == 0), stop=(b == PASSES - 1),
                )
            nc.vector.tensor_scalar(
                out=scores[c][:, half * HALF : (half + 1) * HALF], in0=score[:],
                scalar1=1.0, scalar2=(top[:, c, half - 1 : half] if half > 0 else None),
                op0=ALU.mult, op1=ALU.max, accum_out=top[:, c, half : half + 1],
            )

        def latin_look(c):
            nc.gpsimd.tensor_scalar(
                out=bias[:, c : c + 1], in0=top[:, c, HALVES - 1 : HALVES],
                scalar1=temp_sb[:, c : c + 1], scalar2=-1.0, op0=ALU.mult, op1=ALU.mult,
            )
            latin = ring.tile([P, NP], F32, name="latin", bufs=FAMILY_TILES)
            nc.scalar.activation(
                out=latin[:], in_=scores[c][:].indirect(pos1_sb[:]), func=ACT.Exp,
                bias=bias[:, c : c + 1], scale=temp_sb[:, c : c + 1],
            )
            return latin

        def finish(c, latin):
            pieces = 2 if c == FAMILY_TILES - 1 else 1
            width = NP // pieces
            for piece in range(pieces):
                cols = slice(piece * width, (piece + 1) * width)
                picks = pos2_sb[:, piece * width // LIST : (piece + 1) * width // LIST]
                weighted = ring.tile([P, width], F32, name="weighted", bufs=FAMILY_TILES)
                nc.vector.tensor_tensor(weighted[:], scores[c][:].indirect(picks), latin[:, cols], ALU.mult)
                result = ring.tile([P, width], F32, name="result", bufs=FAMILY_TILES + 1)
                nc.scalar.activation(out=result[:], in_=weighted[:], func=ACT.Abs, bias=fam_sb[:, c : c + 1])
                nc.sync.dma_start(out=out[c * P : (c + 1) * P, cols], in_=result[:])

        for a in range(PASSES):
            quantize_w1(0, a)
        gather_words(0)
        deal_w4_scales()
        deal_w4(0)
        gather_words(1)
        slots = [(b, half, t) for b, half in h_keys for t in range(PACK)]
        for key in slots[:SPELL_BANKS]:
            open_spell(key)
        for key in slots[:LATE_BANKS]:
            open_resid(key)
        first_stage(*h_keys[0])
        for a in range(PASSES):
            quantize_w1(1, a)
        deal_w4(1)
        for key in h_keys[1:]:
            first_stage(*key)
        for b in range(PASSES):
            quantize_h(b, 0)
        for b in range(PASSES):
            nc.vector.tensor_copy(v2_w[b][:], tab2_w[b][:].indirect(offs2_sb[:]))
        for b in range(PASSES):
            quantize_h(b, 1)
        for half in range(HALVES):
            for c in range(FAMILY_TILES):
                second_stage(c, half)
        latins = [latin_look(c) for c in range(FAMILY_TILES)]
        for c in range(FAMILY_TILES):
            finish(c, latins[c])
